import numpy as np
import ml_dtypes

BF16 = ml_dtypes.bfloat16


def bf(x):
    return np.asarray(x, np.float32).astype(BF16)


def f32(x):
    return np.asarray(x, np.float32)


def f64(x):
    return np.asarray(x).astype(np.float64)


def striped(idx):
    return np.tile(idx.reshape(-1, 16).T, (8, 1))


S, K, M, N, B, Q = 512, 128, 128, 512, 2, 256


def setup_inputs():
    return {"base": bf(np.random.standard_normal((B, M, S))), "x": bf(np.random.standard_normal((K, N))), "w": bf(np.random.standard_normal((K, M)) / np.sqrt(K)), "c": f32(0.2 + 0.8 * np.random.random_sample((1, S))), "offs": striped(np.random.permutation(S))}


def reference(base, x, w, c, offs):
    idx = offs[:16].T.reshape(-1)
    z = f64(base).copy()
    for i in range(B):
        z[i][:, idx[i * Q : (i + 1) * Q]] = f64(w).T @ f64(x)[:, i * Q : (i + 1) * Q]
    return z * f64(c)

@@ -1,0 +1,60 @@
+import concourse.mybir as mybir
+from concourse.masks import make_identity
+
+BF16, F32, U16 = mybir.dt.bfloat16, mybir.dt.float32, mybir.dt.uint16
+
+P = 128
+TOKENS = 512
+SEQS = 2
+PIECE = 256
+PIECE_COLS = PIECE // 16
+
+FLOPS = 2 * P * P * SEQS * PIECE
+
+
+def tile_scatter_matmul_kernel(tc, base, x, w, c, offs, out):
+    nc = tc.nc
+    with (
+        tc.tile_pool(name="held", bufs=1) as held,
+        tc.psum_pool(name="banks", bufs=1) as banks,
+    ):
+        offsets = held.tile([P, SEQS * PIECE_COLS], U16, name="offsets")
+        nc.sync.dma_start(offsets[:], offs)
+
+        base_tiles = []
+        for i in range(SEQS):
+            base_tile = held.tile([P, TOKENS], BF16, name="base%d" % i)
+            nc.scalar.dma_start(base_tile[:], base[i])
+            base_tiles.append(base_tile)
+
+        weights = held.tile([P, P], BF16, name="weights")
+        nc.sync.dma_start(weights[:], w)
+        moving = held.tile([P, SEQS * PIECE], BF16, name="moving")
+        nc.sync.dma_start(moving[:], x)
+
+        factors = held.tile([P, TOKENS], F32, name="factors")
+        nc.sync.dma_start(factors[:], c.partition_broadcast(P))
+
+        identity = held.tile([P, P], BF16, name="identity")
+        make_identity(nc, identity[:])
+
+        windows = []
+        for i in range(SEQS):
+            window = banks.tile([P, TOKENS], F32, name="window%d" % i)
+            nc.tensor.matmul(window[:], identity[:], base_tiles[i][:], start=True, stop=True)
+            windows.append(window)
+
+        for i in range(SEQS):
+            nc.tensor.matmul(
+                windows[i][:].indirect(offsets[:, i * PIECE_COLS : (i + 1) * PIECE_COLS]),
+                weights[:],
+                moving[:, i * PIECE : (i + 1) * PIECE],
+                start=True,
+                stop=True,
+            )
+
+        for i in range(SEQS):
+            scaled = held.tile([P, TOKENS], F32, name="scaled%d" % i)
+            nc.vector.tensor_tensor(scaled[:], windows[i][:], factors[:], mybir.AluOpType.mult)
+            store_queue = nc.sync if i % 2 == 0 else nc.scalar
+            store_queue.dma_start(out[i], scaled[:])

@@ -8,6 +8,7 @@ TOKENS = 512
 SEQS = 2
 PIECE = 256
 PIECE_COLS = PIECE // 16
+HALF = TOKENS // 2
 
 FLOPS = 2 * P * P * SEQS * PIECE
 
@@ -54,7 +55,11 @@ def tile_scatter_matmul_kernel(tc, base, x, w, c, offs, out):
             )
 
         for i in range(SEQS):
-            scaled = held.tile([P, TOKENS], F32, name="scaled%d" % i)
-            nc.vector.tensor_tensor(scaled[:], windows[i][:], factors[:], mybir.AluOpType.mult)
-            store_queue = nc.sync if i % 2 == 0 else nc.scalar
-            store_queue.dma_start(out[i], scaled[:])
+            for h in range(2):
+                cols = slice(h * HALF, (h + 1) * HALF)
+                scaled = held.tile([P, HALF], F32, name="scaled%d_%d" % (i, h))
+                nc.vector.tensor_tensor(
+                    scaled[:], windows[i][:, cols], factors[:, cols], mybir.AluOpType.mult
+                )
+                store_queue = nc.sync if h == 0 else nc.scalar
+                store_queue.dma_start(out[i][:, cols], scaled[:])

@@ -8,7 +8,7 @@ TOKENS = 512
 SEQS = 2
 PIECE = 256
 PIECE_COLS = PIECE // 16
-HALF = TOKENS // 2
+WARM_MATMULS = 3
 
 FLOPS = 2 * P * P * SEQS * PIECE
 
@@ -39,6 +39,12 @@ def tile_scatter_matmul_kernel(tc, base, x, w, c, offs, out):
         identity = held.tile([P, P], BF16, name="identity")
         make_identity(nc, identity[:])
 
+        zeros = held.tile([P, TOKENS], BF16, name="zeros")
+        nc.vector.memset(zeros[:], 0.0)
+        warm_bank = banks.tile([P, TOKENS], F32, name="warm_bank")
+        for r in range(WARM_MATMULS):
+            nc.tensor.matmul(warm_bank[:], zeros[:, 0:P], zeros[:], start=True, stop=True)
+
         windows = []
         for i in range(SEQS):
             window = banks.tile([P, TOKENS], F32, name="window%d" % i)
@@ -55,11 +61,7 @@ def tile_scatter_matmul_kernel(tc, base, x, w, c, offs, out):
             )
 
         for i in range(SEQS):
-            for h in range(2):
-                cols = slice(h * HALF, (h + 1) * HALF)
-                scaled = held.tile([P, HALF], F32, name="scaled%d_%d" % (i, h))
-                nc.vector.tensor_tensor(
-                    scaled[:], windows[i][:, cols], factors[:, cols], mybir.AluOpType.mult
-                )
-                store_queue = nc.sync if h == 0 else nc.scalar
-                store_queue.dma_start(out[i][:, cols], scaled[:])
+            scaled = held.tile([P, TOKENS], F32, name="scaled%d" % i)
+            nc.vector.tensor_tensor(scaled[:], windows[i][:], factors[:], mybir.AluOpType.mult)
+            store_queue = nc.sync if i % 2 == 0 else nc.scalar
+            store_queue.dma_start(out[i], scaled[:])

@@ -8,7 +8,6 @@ TOKENS = 512
 SEQS = 2
 PIECE = 256
 PIECE_COLS = PIECE // 16
-WARM_MATMULS = 3
 
 FLOPS = 2 * P * P * SEQS * PIECE
 
@@ -19,31 +18,23 @@ def tile_scatter_matmul_kernel(tc, base, x, w, c, offs, out):
         tc.tile_pool(name="held", bufs=1) as held,
         tc.psum_pool(name="banks", bufs=1) as banks,
     ):
-        offsets = held.tile([P, SEQS * PIECE_COLS], U16, name="offsets")
-        nc.sync.dma_start(offsets[:], offs)
+        factors = held.tile([P, TOKENS], F32, name="factors")
+        nc.scalar.dma_start(factors[:], c.partition_broadcast(P))
 
         base_tiles = []
         for i in range(SEQS):
             base_tile = held.tile([P, TOKENS], BF16, name="base%d" % i)
-            nc.scalar.dma_start(base_tile[:], base[i])
+            nc.sync.dma_start(base_tile[:], base[i])
             base_tiles.append(base_tile)
-
+        offsets = held.tile([P, SEQS * PIECE_COLS], U16, name="offsets")
+        nc.sync.dma_start(offsets[:], offs)
         weights = held.tile([P, P], BF16, name="weights")
         nc.sync.dma_start(weights[:], w)
         moving = held.tile([P, SEQS * PIECE], BF16, name="moving")
         nc.sync.dma_start(moving[:], x)
 
-        factors = held.tile([P, TOKENS], F32, name="factors")
-        nc.sync.dma_start(factors[:], c.partition_broadcast(P))
-
         identity = held.tile([P, P], BF16, name="identity")
         make_identity(nc, identity[:])
-
-        zeros = held.tile([P, TOKENS], BF16, name="zeros")
-        nc.vector.memset(zeros[:], 0.0)
-        warm_bank = banks.tile([P, TOKENS], F32, name="warm_bank")
-        for r in range(WARM_MATMULS):
-            nc.tensor.matmul(warm_bank[:], zeros[:, 0:P], zeros[:], start=True, stop=True)
 
         windows = []
         for i in range(SEQS):

@@ -18,20 +18,21 @@ def tile_scatter_matmul_kernel(tc, base, x, w, c, offs, out):
         tc.tile_pool(name="held", bufs=1) as held,
         tc.psum_pool(name="banks", bufs=1) as banks,
     ):
-        factors = held.tile([P, TOKENS], F32, name="factors")
-        nc.scalar.dma_start(factors[:], c.partition_broadcast(P))
+        offsets = held.tile([P, SEQS * PIECE_COLS], U16, name="offsets")
+        nc.sync.dma_start(offsets[:], offs)
 
         base_tiles = []
         for i in range(SEQS):
             base_tile = held.tile([P, TOKENS], BF16, name="base%d" % i)
-            nc.sync.dma_start(base_tile[:], base[i])
+            nc.scalar.dma_start(base_tile[:], base[i])
             base_tiles.append(base_tile)
-        offsets = held.tile([P, SEQS * PIECE_COLS], U16, name="offsets")
-        nc.sync.dma_start(offsets[:], offs)
-        weights = held.tile([P, P], BF16, name="weights")
-        nc.sync.dma_start(weights[:], w)
         moving = held.tile([P, SEQS * PIECE], BF16, name="moving")
         nc.sync.dma_start(moving[:], x)
+        weights = held.tile([P, P], BF16, name="weights")
+        nc.scalar.dma_start(weights[:], w)
+
+        factors = held.tile([P, TOKENS], F32, name="factors")
+        nc.sync.dma_start(factors[:], c.partition_broadcast(P))
 
         identity = held.tile([P, P], BF16, name="identity")
         make_identity(nc, identity[:])

@@ -18,6 +18,9 @@ def tile_scatter_matmul_kernel(tc, base, x, w, c, offs, out):
         tc.tile_pool(name="held", bufs=1) as held,
         tc.psum_pool(name="banks", bufs=1) as banks,
     ):
+        factor_row = held.tile([1, TOKENS], F32, name="factor_row")
+        nc.sync.dma_start(factor_row[:], c)
+
         offsets = held.tile([P, SEQS * PIECE_COLS], U16, name="offsets")
         nc.sync.dma_start(offsets[:], offs)
 
@@ -31,11 +34,15 @@ def tile_scatter_matmul_kernel(tc, base, x, w, c, offs, out):
         weights = held.tile([P, P], BF16, name="weights")
         nc.scalar.dma_start(weights[:], w)
 
-        factors = held.tile([P, TOKENS], F32, name="factors")
-        nc.sync.dma_start(factors[:], c.partition_broadcast(P))
-
         identity = held.tile([P, P], BF16, name="identity")
         make_identity(nc, identity[:])
+
+        ones_row = held.tile([1, P], F32, name="ones_row")
+        nc.vector.memset(ones_row[:], 1.0)
+        factor_bank = banks.tile([P, TOKENS], F32, name="factor_bank")
+        nc.tensor.matmul(factor_bank[:], ones_row[:], factor_row[:], start=True, stop=True)
+        factors = held.tile([P, TOKENS], F32, name="factors")
+        nc.vector.tensor_copy(factors[:], factor_bank[:])
 
         windows = []
         for i in range(SEQS):

@@ -8,6 +8,7 @@ TOKENS = 512
 SEQS = 2
 PIECE = 256
 PIECE_COLS = PIECE // 16
+WARM_UPS = 4
 
 FLOPS = 2 * P * P * SEQS * PIECE
 
@@ -33,6 +34,12 @@ def tile_scatter_matmul_kernel(tc, base, x, w, c, offs, out):
         nc.sync.dma_start(moving[:], x)
         weights = held.tile([P, P], BF16, name="weights")
         nc.scalar.dma_start(weights[:], w)
+
+        zeros = held.tile([P, TOKENS], BF16, name="zeros")
+        nc.vector.memset(zeros[:], 0.0)
+        unread_bank = banks.tile([P, TOKENS], F32, name="unread_bank")
+        for warm_up in range(WARM_UPS):
+            nc.tensor.matmul(unread_bank[:], zeros[:, 0:P], zeros[:], start=True, stop=True)
 
         identity = held.tile([P, P], BF16, name="identity")
         make_identity(nc, identity[:])

@@ -8,7 +8,10 @@ TOKENS = 512
 SEQS = 2
 PIECE = 256
 PIECE_COLS = PIECE // 16
-WARM_UPS = 4
+BLOCK = 32
+C_ROWS = TOKENS // BLOCK
+QUADRANTS = P // BLOCK
+WARM_UPS = 3
 
 FLOPS = 2 * P * P * SEQS * PIECE
 
@@ -19,8 +22,13 @@ def tile_scatter_matmul_kernel(tc, base, x, w, c, offs, out):
         tc.tile_pool(name="held", bufs=1) as held,
         tc.psum_pool(name="banks", bufs=1) as banks,
     ):
-        factor_row = held.tile([1, TOKENS], F32, name="factor_row")
-        nc.sync.dma_start(factor_row[:], c)
+        c_rows = held.tile([C_ROWS, QUADRANTS, BLOCK], F32, name="c_rows")
+        nc.sync.dma_start(
+            c_rows[:],
+            c.rearrange("o (r j) -> (o r) j", j=BLOCK)
+            .unsqueeze(1)
+            .to_broadcast([C_ROWS, QUADRANTS, BLOCK]),
+        )
 
         offsets = held.tile([P, SEQS * PIECE_COLS], U16, name="offsets")
         nc.sync.dma_start(offsets[:], offs)
@@ -43,13 +51,23 @@ def tile_scatter_matmul_kernel(tc, base, x, w, c, offs, out):
 
         identity = held.tile([P, P], BF16, name="identity")
         make_identity(nc, identity[:])
+        small_identity = held.tile([C_ROWS, C_ROWS], F32, name="small_identity")
+        make_identity(nc, small_identity[:])
 
-        ones_row = held.tile([1, P], F32, name="ones_row")
-        nc.vector.memset(ones_row[:], 1.0)
-        factor_bank = banks.tile([P, TOKENS], F32, name="factor_bank")
-        nc.tensor.matmul(factor_bank[:], ones_row[:], factor_row[:], start=True, stop=True)
-        factors = held.tile([P, TOKENS], F32, name="factors")
-        nc.vector.tensor_copy(factors[:], factor_bank[:])
+        c_columns = banks.tile([P, C_ROWS], F32, name="c_columns")
+        nc.tensor.matmul(
+            c_columns[:],
+            c_rows[:].rearrange("r q j -> r (q j)"),
+            small_identity[:],
+            start=True,
+            stop=True,
+        )
+        spread = held.tile([P, C_ROWS, BLOCK], F32, name="spread", align_bytes=64)
+        nc.vector.tensor_copy(
+            spread[:], c_columns[:].unsqueeze(2).to_broadcast([P, C_ROWS, BLOCK])
+        )
+        factors = held.tile([P, TOKENS], F32, name="factors", align_bytes=64)
+        nc.vector.transpose(factors[:], spread[:].rearrange("p r n -> p (r n)"))
 
         windows = []
         for i in range(SEQS):

@@ -22,13 +22,14 @@ def tile_scatter_matmul_kernel(tc, base, x, w, c, offs, out):
         tc.tile_pool(name="held", bufs=1) as held,
         tc.psum_pool(name="banks", bufs=1) as banks,
     ):
-        c_rows = held.tile([C_ROWS, QUADRANTS, BLOCK], F32, name="c_rows")
-        nc.sync.dma_start(
-            c_rows[:],
-            c.rearrange("o (r j) -> (o r) j", j=BLOCK)
-            .unsqueeze(1)
-            .to_broadcast([C_ROWS, QUADRANTS, BLOCK]),
-        )
+        c_rows = held.tile([P, BLOCK], F32, name="c_rows", align_bytes=64)
+        nc.gpsimd.memset(c_rows[:], 0.0)
+        for q in range(QUADRANTS):
+            load_queue = nc.sync if q % 2 == 0 else nc.scalar
+            load_queue.dma_start(
+                c_rows[q * BLOCK : q * BLOCK + C_ROWS, :],
+                c.rearrange("o (r j) -> (o r) j", j=BLOCK),
+            )
 
         offsets = held.tile([P, SEQS * PIECE_COLS], U16, name="offsets")
         nc.sync.dma_start(offsets[:], offs)
@@ -51,20 +52,12 @@ def tile_scatter_matmul_kernel(tc, base, x, w, c, offs, out):
 
         identity = held.tile([P, P], BF16, name="identity")
         make_identity(nc, identity[:])
-        small_identity = held.tile([C_ROWS, C_ROWS], F32, name="small_identity")
-        make_identity(nc, small_identity[:])
 
-        c_columns = banks.tile([P, C_ROWS], F32, name="c_columns")
-        nc.tensor.matmul(
-            c_columns[:],
-            c_rows[:].rearrange("r q j -> r (q j)"),
-            small_identity[:],
-            start=True,
-            stop=True,
-        )
+        c_columns = held.tile([P, BLOCK], F32, name="c_columns", align_bytes=64)
+        nc.vector.transpose(c_columns[:], c_rows[:])
         spread = held.tile([P, C_ROWS, BLOCK], F32, name="spread", align_bytes=64)
         nc.vector.tensor_copy(
-            spread[:], c_columns[:].unsqueeze(2).to_broadcast([P, C_ROWS, BLOCK])
+            spread[:], c_columns[:, 0:C_ROWS].unsqueeze(2).to_broadcast([P, C_ROWS, BLOCK])
         )
         factors = held.tile([P, TOKENS], F32, name="factors", align_bytes=64)
         nc.vector.transpose(factors[:], spread[:].rearrange("p r n -> p (r n)"))

@@ -77,8 +77,11 @@ def tile_scatter_matmul_kernel(tc, base, x, w, c, offs, out):
                 stop=True,
             )
 
-        for i in range(SEQS):
-            scaled = held.tile([P, TOKENS], F32, name="scaled%d" % i)
-            nc.vector.tensor_tensor(scaled[:], windows[i][:], factors[:], mybir.AluOpType.mult)
-            store_queue = nc.sync if i % 2 == 0 else nc.scalar
-            store_queue.dma_start(out[i], scaled[:])
+        pieces = [(0, 0, TOKENS), (1, 0, TOKENS // 2), (1, TOKENS // 2, TOKENS)]
+        for n, (i, first, last) in enumerate(pieces):
+            scaled = held.tile([P, last - first], F32, name="scaled%d" % n)
+            nc.vector.tensor_tensor(
+                scaled[:], windows[i][:, first:last], factors[:, first:last], mybir.AluOpType.mult
+            )
+            store_queue = nc.sync if n % 2 == 0 else nc.scalar
+            store_queue.dma_start(out[i][:, first:last], scaled[:])

@@ -23,13 +23,13 @@ def tile_scatter_matmul_kernel(tc, base, x, w, c, offs, out):
         tc.psum_pool(name="banks", bufs=1) as banks,
     ):
         c_rows = held.tile([P, BLOCK], F32, name="c_rows", align_bytes=64)
-        nc.gpsimd.memset(c_rows[:], 0.0)
         for q in range(QUADRANTS):
             load_queue = nc.sync if q % 2 == 0 else nc.scalar
             load_queue.dma_start(
-                c_rows[q * BLOCK : q * BLOCK + C_ROWS, :],
+                c_rows[q * BLOCK + C_ROWS : (q + 1) * BLOCK, :],
                 c.rearrange("o (r j) -> (o r) j", j=BLOCK),
             )
+            nc.gpsimd.memset(c_rows[q * BLOCK : q * BLOCK + C_ROWS, :], 0.0)
 
         offsets = held.tile([P, SEQS * PIECE_COLS], U16, name="offsets")
         nc.sync.dma_start(offsets[:], offs)
@@ -57,7 +57,7 @@ def tile_scatter_matmul_kernel(tc, base, x, w, c, offs, out):
         nc.vector.transpose(c_columns[:], c_rows[:])
         spread = held.tile([P, C_ROWS, BLOCK], F32, name="spread", align_bytes=64)
         nc.vector.tensor_copy(
-            spread[:], c_columns[:, 0:C_ROWS].unsqueeze(2).to_broadcast([P, C_ROWS, BLOCK])
+            spread[:], c_columns[:, C_ROWS:BLOCK].unsqueeze(2).to_broadcast([P, C_ROWS, BLOCK])
         )
         factors = held.tile([P, TOKENS], F32, name="factors", align_bytes=64)
         nc.vector.transpose(factors[:], spread[:].rearrange("p r n -> p (r n)"))

@@ -22,6 +22,9 @@ def tile_scatter_matmul_kernel(tc, base, x, w, c, offs, out):
         tc.tile_pool(name="held", bufs=1) as held,
         tc.psum_pool(name="banks", bufs=1) as banks,
     ):
+        zeros = held.tile([P, TOKENS], BF16, name="zeros")
+        nc.vector.memset(zeros[:], 0.0)
+
         c_rows = held.tile([P, BLOCK], F32, name="c_rows", align_bytes=64)
         for q in range(QUADRANTS):
             load_queue = nc.sync if q % 2 == 0 else nc.scalar
@@ -29,7 +32,7 @@ def tile_scatter_matmul_kernel(tc, base, x, w, c, offs, out):
                 c_rows[q * BLOCK + C_ROWS : (q + 1) * BLOCK, :],
                 c.rearrange("o (r j) -> (o r) j", j=BLOCK),
             )
-            nc.gpsimd.memset(c_rows[q * BLOCK : q * BLOCK + C_ROWS, :], 0.0)
+            nc.vector.memset(c_rows[q * BLOCK : q * BLOCK + C_ROWS, :], 0.0)
 
         offsets = held.tile([P, SEQS * PIECE_COLS], U16, name="offsets")
         nc.sync.dma_start(offsets[:], offs)
@@ -44,8 +47,6 @@ def tile_scatter_matmul_kernel(tc, base, x, w, c, offs, out):
         weights = held.tile([P, P], BF16, name="weights")
         nc.scalar.dma_start(weights[:], w)
 
-        zeros = held.tile([P, TOKENS], BF16, name="zeros")
-        nc.vector.memset(zeros[:], 0.0)
         unread_bank = banks.tile([P, TOKENS], F32, name="unread_bank")
         for warm_up in range(WARM_UPS):
             nc.tensor.matmul(unread_bank[:], zeros[:, 0:P], zeros[:], start=True, stop=True)

import concourse.mybir as mybir
from concourse.masks import make_identity

BF16, F32, U16 = mybir.dt.bfloat16, mybir.dt.float32, mybir.dt.uint16

P = 128
TOKENS = 512
SEQS = 2
PIECE = 256
PIECE_COLS = PIECE // 16
BLOCK = 32
C_ROWS = TOKENS // BLOCK
QUADRANTS = P // BLOCK
WARM_UPS = 3

FLOPS = 2 * P * P * SEQS * PIECE


def tile_scatter_matmul_kernel(tc, base, x, w, c, offs, out):
    nc = tc.nc
    with (
        tc.tile_pool(name="held", bufs=1) as held,
        tc.psum_pool(name="banks", bufs=1) as banks,
    ):
        zeros = held.tile([P, TOKENS], BF16, name="zeros")
        nc.vector.memset(zeros[:], 0.0)

        c_rows = held.tile([P, BLOCK], F32, name="c_rows", align_bytes=64)
        for q in range(QUADRANTS):
            load_queue = nc.sync if q % 2 == 0 else nc.scalar
            load_queue.dma_start(
                c_rows[q * BLOCK + C_ROWS : (q + 1) * BLOCK, :],
                c.rearrange("o (r j) -> (o r) j", j=BLOCK),
            )
            nc.vector.memset(c_rows[q * BLOCK : q * BLOCK + C_ROWS, :], 0.0)

        offsets = held.tile([P, SEQS * PIECE_COLS], U16, name="offsets")
        nc.sync.dma_start(offsets[:], offs)

        base_tiles = []
        for i in range(SEQS):
            base_tile = held.tile([P, TOKENS], BF16, name="base%d" % i)
            nc.scalar.dma_start(base_tile[:], base[i])
            base_tiles.append(base_tile)
        moving = held.tile([P, SEQS * PIECE], BF16, name="moving")
        nc.sync.dma_start(moving[:], x)
        weights = held.tile([P, P], BF16, name="weights")
        nc.scalar.dma_start(weights[:], w)

        unread_bank = banks.tile([P, TOKENS], F32, name="unread_bank")
        for warm_up in range(WARM_UPS):
            nc.tensor.matmul(unread_bank[:], zeros[:, 0:P], zeros[:], start=True, stop=True)

        identity = held.tile([P, P], BF16, name="identity")
        make_identity(nc, identity[:])

        c_columns = held.tile([P, BLOCK], F32, name="c_columns", align_bytes=64)
        nc.vector.transpose(c_columns[:], c_rows[:])
        spread = held.tile([P, C_ROWS, BLOCK], F32, name="spread", align_bytes=64)
        nc.vector.tensor_copy(
            spread[:], c_columns[:, C_ROWS:BLOCK].unsqueeze(2).to_broadcast([P, C_ROWS, BLOCK])
        )
        factors = held.tile([P, TOKENS], F32, name="factors", align_bytes=64)
        nc.vector.transpose(factors[:], spread[:].rearrange("p r n -> p (r n)"))

        windows = []
        for i in range(SEQS):
            window = banks.tile([P, TOKENS], F32, name="window%d" % i)
            nc.tensor.matmul(window[:], identity[:], base_tiles[i][:], start=True, stop=True)
            windows.append(window)

        for i in range(SEQS):
            nc.tensor.matmul(
                windows[i][:].indirect(offsets[:, i * PIECE_COLS : (i + 1) * PIECE_COLS]),
                weights[:],
                moving[:, i * PIECE : (i + 1) * PIECE],
                start=True,
                stop=True,
            )

        pieces = [(0, 0, TOKENS), (1, 0, TOKENS // 2), (1, TOKENS // 2, TOKENS)]
        for n, (i, first, last) in enumerate(pieces):
            scaled = held.tile([P, last - first], F32, name="scaled%d" % n)
            nc.vector.tensor_tensor(
                scaled[:], windows[i][:, first:last], factors[:, first:last], mybir.AluOpType.mult
            )
            store_queue = nc.sync if n % 2 == 0 else nc.scalar
            store_queue.dma_start(out[i][:, first:last], scaled[:])
